import numpy as np
import ml_dtypes


def mxq(x, axis, fmt="e4m3"):
    dtype, down = {"e4m3": (ml_dtypes.float8_e4m3fn, 7), "e5m2": (ml_dtypes.float8_e5m2, 14)}[fmt]
    v = np.moveaxis(np.asarray(x, np.float32).astype(ml_dtypes.bfloat16).astype(np.float64), axis, -1)
    blocks = v.reshape(v.shape[:-1] + (-1, 32))
    amax = np.abs(blocks).max(-1, keepdims=True)
    byte = np.maximum(np.where(amax > 0, np.frexp(amax)[1] - 1 + 127, 0) - down, 1)
    scale = np.exp2(byte - 127.0)
    codes = (blocks / scale).astype(np.float32).astype(dtype).astype(np.float64)
    return np.moveaxis((codes * scale).reshape(v.shape), -1, axis)


WIDE = False


def mx_kscale(k):
    if not WIDE:
        return np.ones(k)
    levels = np.array([30, -30])
    if k % 512:
        return np.exp2(np.random.permutation(np.resize(levels, k // 32))).repeat(32)
    a = np.empty((k // 512, 16))
    for p in range(k // 512):
        a[p, :8] = np.random.permutation(np.resize(levels, 8))
        for g in range(8):
            far = levels[np.abs(levels - a[p, g]) >= 10]
            a[p, g + 8] = far[np.random.randint(len(far))]
    return np.exp2(a.ravel()).repeat(32)


def f64(x):
    return np.asarray(x).astype(np.float64)


def striped(idx):
    return np.tile(np.asarray(idx).reshape(-1, 16).T, (8, 1)).astype(np.uint16)


def unstriped(offs):
    return offs[:16].T.reshape(-1).astype(np.int64)


E2M1 = np.array([0.0, 0.5, 1.0, 1.5, 2.0, 3.0, 4.0, 6.0, -0.0, -0.5, -1.0, -1.5, -2.0, -3.0, -4.0, -6.0])


def pack_weight(w, fmt):
    k, n = w.shape
    w = f64(np.asarray(w, np.float32).astype(ml_dtypes.bfloat16)).reshape(k // 32, 32, n)
    amax = np.abs(w).max(1)
    if fmt in ("e4m3", "e5m2"):
        byte = np.frexp(amax)[1] - 1 + 127 - (7 if fmt == "e4m3" else 14)
    else:
        mant, ex = np.frexp(amax / 6.0)
        byte = np.where(mant > 0.5, ex, ex - 1) + 127
    byte = np.clip(np.where(amax > 0, byte, 1), 1, 254)
    scaled = (w * np.exp2(127.0 - byte)[:, None, :]).reshape(k, n).astype(np.float32)
    by_word = np.ascontiguousarray(scaled.reshape(k // 512, 128, 4, n).transpose(0, 1, 3, 2))
    if fmt in ("e4m3", "e5m2"):
        words = by_word.astype(ml_dtypes.float8_e4m3fn if fmt == "e4m3" else ml_dtypes.float8_e5m2).view(np.uint8)
    else:
        c = by_word.astype(ml_dtypes.float4_e2m1fn).view(np.uint8) & 0xF
        words = (c[..., 0::2] | (c[..., 1::2] << 4)).reshape(k // 512, 128, 2 * n)
    return np.ascontiguousarray(words), np.ascontiguousarray(byte.astype(np.uint8).reshape(k // 512, 16, n))


def unpack_weight(words, scales, fmt):
    g, _, n = scales.shape
    words = np.ascontiguousarray(words).reshape(g, 128, n, -1)
    if fmt in ("e4m3", "e5m2"):
        vals = words.view(ml_dtypes.float8_e4m3fn if fmt == "e4m3" else ml_dtypes.float8_e5m2).astype(np.float64)
    else:
        nib = np.empty((g, 128, n, 4), np.uint8)
        nib[..., 0::2] = words & 0xF
        nib[..., 1::2] = words >> 4
        vals = E2M1[nib]
    vals = vals * np.repeat(np.exp2(scales.astype(np.float64) - 127.0), 8, axis=1)[..., None]
    return vals.transpose(0, 1, 3, 2).reshape(g * 512, n)


def sigmoid(v):
    return 1.0 / (1.0 + np.exp(-v))


K, T, Z, J, R, Q, N, E = 512, 1024, 1024, 256, 512, 1024, 256, 128


def setup_inputs():
    n = np.random.standard_normal
    idx = np.random.permutation(T)[:J]
    idx2 = np.random.permutation(Z)[:J]
    idx3 = np.random.permutation(Q)[:J]
    idx4 = np.random.permutation(J)[:E]
    idx5 = np.random.permutation(J)[:E]
    fk = mx_kscale(K)
    fr = mx_kscale(R)
    xtp = pack_weight(n((K, T)) / fk[:, None], "e2m1")
    xop = pack_weight(n((K, Z)) / fk[:, None], "e4m3")
    wp = pack_weight(n((K, R)) * 1 / np.sqrt(K) * fk[:, None] * fr, "e4m3")
    w2p = pack_weight(n((K, R)) * 1 / np.sqrt(K) * fk[:, None] * fr, "e5m2")
    wbp = pack_weight(n((R, N)) * 1 / np.sqrt(R) / fr[:, None], "e2m1")
    return {
        "xt_words": xtp[0],
        "xt_scales": xtp[1],
        "xo_words": xop[0],
        "xo_scales": xop[1],
        "w_words": wp[0],
        "w_scales": wp[1],
        "w2_words": w2p[0],
        "w2_scales": w2p[1],
        "tg": (1.0 * n((R, Q))).astype(np.float32),
        "sg": (np.random.uniform(0.6, 1.6, (R, 1))).astype(np.float32),
        "bg": (np.random.uniform(-1.0, 1.0, (R, 1))).astype(np.float32),
        "wb_words": wbp[0],
        "wb_scales": wbp[1],
        "offs": striped(idx),
        "offs2": striped(idx2),
        "offs3": striped(idx3),
        "offs4": striped(idx4),
        "offs5": striped(idx5),
    }


def reference(xt_words, xt_scales, xo_words, xo_scales, w_words, w_scales, w2_words, w2_scales, tg, sg, bg, wb_words, wb_scales, offs, offs2, offs3, offs4, offs5):
    idx = unstriped(offs)
    idx2 = unstriped(offs2)
    idx3 = unstriped(offs3)
    idx4 = unstriped(offs4)
    idx5 = unstriped(offs5)
    xtu = unpack_weight(xt_words, xt_scales, "e2m1")
    xou = unpack_weight(xo_words, xo_scales, "e4m3")
    wu = unpack_weight(w_words, w_scales, "e4m3")
    w2u = unpack_weight(w2_words, w2_scales, "e5m2")
    wbu = unpack_weight(wb_words, wb_scales, "e2m1")
    xtidxg = xtu[:, idx]
    xoidx2g = xou[:, idx2]
    a = wu.T @ xtidxg + w2u.T @ xoidx2g
    b = w2u.T @ xtidxg + wu.T @ xoidx2g
    hid = np.maximum(a, b) * sigmoid(f64(tg)[:, idx3] * f64(sg) + f64(bg))
    hidq = mxq(hid, 0, "e5m2")
    p = wbu.T @ hidq
    y = np.maximum(p[:, idx4], p[:, idx5])
    return y

@@ -1,0 +1,206 @@
+from contextlib import ExitStack
+
+import concourse.mybir as mybir
+
+F32 = mybir.dt.float32
+BF16 = mybir.dt.bfloat16
+I32 = mybir.dt.int32
+U32 = mybir.dt.uint32
+U16 = mybir.dt.uint16
+U8 = mybir.dt.uint8
+E4M3 = mybir.dt.float8_e4m3fn_x4
+E5M2 = mybir.dt.float8_e5m2_x4
+E2M1 = mybir.dt.float4_e2m1fn_x4
+ACT = mybir.ActivationFunctionType
+ALU = mybir.AluOpType
+
+K, T, Z, J, R, Q, N, E = 512, 1024, 1024, 256, 512, 1024, 256, 128
+P = 128
+PACK = 4
+JH = J // 2
+
+FLOPS = 2 * (4 * K * R * J + R * N * J)
+
+
+def tile_list_crossed_tablegate_one_bestoftwo_kernel(
+    tc, xt_words, xt_scales, xo_words, xo_scales, w_words, w_scales, w2_words, w2_scales,
+    tg, sg, bg, wb_words, wb_scales, offs, offs2, offs3, offs4, offs5, out,
+):
+    nc = tc.nc
+    with ExitStack() as ctx:
+        lists = ctx.enter_context(tc.tile_pool(name="lists", bufs=1))
+        sb = ctx.enter_context(tc.tile_pool(name="sb", bufs=1))
+        psum = ctx.enter_context(tc.psum_pool(name="psum", bufs=1))
+
+        def load_list(src, name):
+            tile = lists.tile(list(src.shape), U16, name=name)
+            nc.sync.dma_start(tile[:], src)
+            return tile
+
+        def scale_plane(width, name):
+            plane = sb.tile([P, width], U8, name=name, align_bytes=64)
+            nc.vector.memset(plane[:].bitcast(I32), 0)
+            return plane
+
+        def load_scales(queue, plane, src, quads=range(4)):
+            for quad in quads:
+                queue.dma_start(
+                    plane[32 * quad : 32 * quad + 4, :].bitcast(I32),
+                    src[0, 4 * quad : 4 * quad + 4, :].bitcast(I32),
+                )
+
+        def load_words(queue, width, dtype, src, name):
+            tile = sb.tile([P, width], dtype, name=name, align_bytes=64)
+            queue.dma_start(tile[:].bitcast(I32), src.bitcast(I32))
+            return tile
+
+        def words32(src):
+            return src[0].rearrange("p c b -> p (c b)")
+
+        tg_rows = tg.rearrange("(p t) q -> p t q", t=PACK)
+        tg_sb = [None] * PACK
+
+        def load_tg(queue, t):
+            tg_sb[t] = sb.tile([P, Q], F32, name="tg%d" % t)
+            queue.dma_start(tg_sb[t][:], tg_rows[:, t, :])
+
+        def load_col(queue, src, name):
+            tile = sb.tile([P, PACK], F32, name=name)
+            queue.dma_start(tile[:], src.rearrange("(p t) o -> p (t o)", t=PACK))
+            return tile
+
+        xt_s = scale_plane(T, "xt_s")
+        w_s_raw = scale_plane(R, "w_s_raw")
+        w2_s_raw = scale_plane(R, "w2_s_raw")
+        xo_s = scale_plane(Z, "xo_s")
+        wb_s = scale_plane(N, "wb_s")
+
+        idx = load_list(offs, "idx")
+        xt_w = load_words(nc.sync, T, U16, xt_words[0], "xt_w")
+        load_scales(nc.gpsimd, w2_s_raw, w2_scales)
+        sg_sb = load_col(nc.gpsimd, sg, "sg_sb")
+        bg_sb = load_col(nc.gpsimd, bg, "bg_sb")
+        load_scales(nc.sync, xt_s, xt_scales, (0, 1))
+        w_w_raw = load_words(nc.sync, R, U32, words32(w_words), "w_w_raw")
+        load_scales(nc.sync, xt_s, xt_scales, (2, 3))
+        xo_w = load_words(nc.sync, Z, U32, words32(xo_words), "xo_w")
+        load_scales(nc.sync, w_s_raw, w_scales, (0, 1))
+        w2_w_raw = load_words(nc.sync, R, U32, words32(w2_words), "w2_w_raw")
+        load_scales(nc.sync, w_s_raw, w_scales, (2, 3))
+        load_tg(nc.sync, 0)
+        idx2 = load_list(offs2, "idx2")
+        load_scales(nc.sync, xo_s, xo_scales, (0, 1))
+        load_tg(nc.sync, 1)
+        load_scales(nc.sync, xo_s, xo_scales, (2, 3))
+        idx3 = load_list(offs3, "idx3")
+        load_tg(nc.sync, 2)
+        load_tg(nc.sync, 3)
+        wb_w = load_words(nc.sync, 2 * N, U8, wb_words[0], "wb_w")
+        load_scales(nc.sync, wb_s, wb_scales)
+        idx4 = load_list(offs4, "idx4")
+        idx5 = load_list(offs5, "idx5")
+
+        def gather(table, offsets, dtype, name):
+            picked = sb.tile([P, J], dtype, name=name, align_bytes=64)
+            nc.vector.tensor_copy(picked[:], table[:].indirect(offsets[:]))
+            return picked
+
+        def deal(raw, dtype, name, tag=None):
+            dealt = sb.tile([P, R], dtype, name=name, tag=tag or name, align_bytes=64)
+            nc.vector.tensor_copy(
+                dealt[:].rearrange("p (t c i) -> p c t i", t=PACK, i=4),
+                raw[:].rearrange("p (c i t) -> p c t i", t=PACK, i=4),
+            )
+            return dealt
+
+        xt_gw = gather(xt_w, idx, U16, "xt_gw")
+        xt_gs = gather(xt_s, idx, U8, "xt_gs")
+        w_w = deal(w_w_raw, U32, "w_w")
+        w_s = deal(w_s_raw, U8, "w_s")
+        w2_w = deal(w2_w_raw, U32, "w2_w")
+        w2_s = deal(w2_s_raw, U8, "w2_s", tag="w_s_raw")
+        xo_gw = gather(xo_w, idx2, U32, "xo_gw")
+        xo_gs = gather(xo_s, idx2, U8, "xo_gs")
+
+        first = (w_w, w_s, E4M3)
+        second = (w2_w, w2_s, E5M2)
+        tokens = (xt_gw, xt_gs, E2M1)
+        notes = (xo_gw, xo_gs, E4M3)
+
+        def product(acc, weight, t, moving, start):
+            cols = slice(t * P, (t + 1) * P)
+            nc.tensor.matmul_mx(
+                out=acc[:],
+                lhsT=weight[0][:, cols].bitcast(weight[2]),
+                lhsT_scale=weight[1][:, cols],
+                rhs=moving[0][:].bitcast(moving[2]),
+                rhs_scale=moving[1][:],
+                start=start,
+                stop=not start,
+            )
+
+        a_ps = [psum.tile([P, J], F32, name="a%d" % t, tag="bank%d" % t) for t in range(PACK)]
+        b_ps = [psum.tile([P, J], F32, name="b%d" % t, tag="bank%d" % (PACK + t)) for t in range(PACK)]
+        for t in range(PACK):
+            product(a_ps[t], first, t, tokens, True)
+        for t in range(PACK):
+            product(b_ps[t], second, t, tokens, True)
+
+        hid = sb.tile([P, PACK, J], F32, name="hid")
+        for t in range(PACK):
+            product(a_ps[t], second, t, notes, False)
+            product(b_ps[t], first, t, notes, False)
+            a_sb = sb.tile([P, J], F32, name="a_sb%d" % t)
+            nc.scalar.copy(a_sb[:], a_ps[t][:])
+            best = sb.tile([P, J], F32, name="best%d" % t)
+            nc.vector.tensor_tensor(best[:], b_ps[t][:], a_sb[:], ALU.max)
+            gate = sb.tile([P, J], F32, name="gate%d" % t)
+            nc.scalar.activation(
+                out=gate[:], in_=tg_sb[t][:].indirect(idx3[:]), func=ACT.Sigmoid,
+                bias=bg_sb[:, t : t + 1], scale=sg_sb[:, t : t + 1],
+            )
+            nc.vector.tensor_tensor(hid[:, t, :], best[:], gate[:], ALU.mult)
+
+        p_sb = [sb.tile([P, J], F32, name="p_sb%d" % h) for h in range(2)]
+        woven = [sb.tile([P, JH, PACK], BF16, name="woven%d" % s, align_bytes=64) for s in range(2)]
+        for s in range(2):
+            nc.vector.tensor_copy(
+                woven[s][:].rearrange("p (c i) t -> p c t i", i=4),
+                hid[:, :, s * JH : (s + 1) * JH].rearrange("p t (c i) -> p c t i", i=4),
+            )
+        for s in range(2):
+            codes = sb.tile([P, JH], U32, name="codes%d" % s, align_bytes=64)
+            plane = sb.tile([P, JH], U8, name="plane%d" % s, align_bytes=64)
+            nc.vector.quantize_mx(
+                out=codes[:].bitcast(E5M2), scales=plane[:],
+                in_=woven[s][:].rearrange("p j t -> p (j t)"),
+            )
+            for h in range(2):
+                p_ps = psum.tile([P, JH], F32, name="p%d%d" % (s, h), tag="bank%d" % (2 * s + h))
+                nc.tensor.matmul_mx(
+                    out=p_ps[:],
+                    lhsT=wb_w[:, h * 2 * P : (h + 1) * 2 * P].bitcast(E2M1),
+                    lhsT_scale=wb_s[:, h * P : (h + 1) * P],
+                    rhs=codes[:].bitcast(E5M2),
+                    rhs_scale=plane[:],
+                    start=True,
+                    stop=True,
+                )
+                dst = p_sb[h][:, s * JH : (s + 1) * JH]
+                if s == 1 and h == 1:
+                    nc.vector.tensor_copy(dst, p_ps[:])
+                else:
+                    nc.scalar.copy(dst, p_ps[:])
+
+        for h in (1, 0):
+            picks = []
+            for k, offsets in enumerate((idx4, idx5)):
+                pick = sb.tile([P, E], F32, name="pick%d%d" % (h, k))
+                if h == 0:
+                    nc.scalar.activation(out=pick[:], in_=p_sb[h][:].indirect(offsets[:]), func=ACT.Copy)
+                else:
+                    nc.vector.tensor_copy(pick[:], p_sb[h][:].indirect(offsets[:]))
+                picks.append(pick)
+            res = sb.tile([P, E], F32, name="res%d" % h)
+            nc.vector.tensor_tensor(res[:], picks[0][:], picks[1][:], ALU.max)
+            nc.sync.dma_start(out[h * P : (h + 1) * P, :], res[:])

@@ -69,36 +69,38 @@ def tile_list_crossed_tablegate_one_bestoftwo_kernel(
             queue.dma_start(tile[:], src.rearrange("(p t) o -> p (t o)", t=PACK))
             return tile
 
+        w2_s_raw = scale_plane(R, "w2_s_raw")
         xt_s = scale_plane(T, "xt_s")
         w_s_raw = scale_plane(R, "w_s_raw")
-        w2_s_raw = scale_plane(R, "w2_s_raw")
         xo_s = scale_plane(Z, "xo_s")
         wb_s = scale_plane(N, "wb_s")
 
+        load_scales(nc.gpsimd, w2_s_raw, w2_scales)
         idx = load_list(offs, "idx")
         xt_w = load_words(nc.sync, T, U16, xt_words[0], "xt_w")
-        load_scales(nc.gpsimd, w2_s_raw, w2_scales)
-        sg_sb = load_col(nc.gpsimd, sg, "sg_sb")
-        bg_sb = load_col(nc.gpsimd, bg, "bg_sb")
-        load_scales(nc.sync, xt_s, xt_scales, (0, 1))
+        load_scales(nc.sync, xt_s, xt_scales)
         w_w_raw = load_words(nc.sync, R, U32, words32(w_words), "w_w_raw")
-        load_scales(nc.sync, xt_s, xt_scales, (2, 3))
         xo_w = load_words(nc.sync, Z, U32, words32(xo_words), "xo_w")
-        load_scales(nc.sync, w_s_raw, w_scales, (0, 1))
-        w2_w_raw = load_words(nc.sync, R, U32, words32(w2_words), "w2_w_raw")
-        load_scales(nc.sync, w_s_raw, w_scales, (2, 3))
-        load_tg(nc.sync, 0)
+        load_scales(nc.sync, w_s_raw, w_scales)
         idx2 = load_list(offs2, "idx2")
-        load_scales(nc.sync, xo_s, xo_scales, (0, 1))
+        w2_w_raw = load_words(nc.sync, R, U32, words32(w2_words), "w2_w_raw")
+        load_tg(nc.sync, 0)
+        load_scales(nc.sync, xo_s, xo_scales)
         load_tg(nc.sync, 1)
-        load_scales(nc.sync, xo_s, xo_scales, (2, 3))
         idx3 = load_list(offs3, "idx3")
+        sg_sb = load_col(nc.sync, sg, "sg_sb")
+        bg_sb = load_col(nc.sync, bg, "bg_sb")
         load_tg(nc.sync, 2)
         load_tg(nc.sync, 3)
         wb_w = load_words(nc.sync, 2 * N, U8, wb_words[0], "wb_w")
         load_scales(nc.sync, wb_s, wb_scales)
         idx4 = load_list(offs4, "idx4")
         idx5 = load_list(offs5, "idx5")
+
+        warm_in = sb.tile([P, 1], F32, name="warm_in")
+        warm_out = sb.tile([P, 1], F32, name="warm_out")
+        nc.vector.memset(warm_in[:], 0.0)
+        nc.scalar.activation(out=warm_out[:], in_=warm_in[:], func=ACT.Sigmoid)
 
         def gather(table, offsets, dtype, name):
             picked = sb.tile([P, J], dtype, name=name, align_bytes=64)
@@ -117,9 +119,9 @@ def tile_list_crossed_tablegate_one_bestoftwo_kernel(
         xt_gs = gather(xt_s, idx, U8, "xt_gs")
         w_w = deal(w_w_raw, U32, "w_w")
         w_s = deal(w_s_raw, U8, "w_s")
-        w2_w = deal(w2_w_raw, U32, "w2_w")
-        w2_s = deal(w2_s_raw, U8, "w2_s", tag="w_s_raw")
         xo_gw = gather(xo_w, idx2, U32, "xo_gw")
+        w2_w = deal(w2_w_raw, U32, "w2_w")
+        w2_s = deal(w2_s_raw, U8, "w2_s", tag="w2_w_raw")
         xo_gs = gather(xo_s, idx2, U8, "xo_gs")
 
         first = (w_w, w_s, E4M3)
@@ -127,46 +129,49 @@ def tile_list_crossed_tablegate_one_bestoftwo_kernel(
         tokens = (xt_gw, xt_gs, E2M1)
         notes = (xo_gw, xo_gs, E4M3)
 
-        def product(acc, weight, t, moving, start):
-            cols = slice(t * P, (t + 1) * P)
-            nc.tensor.matmul_mx(
-                out=acc[:],
-                lhsT=weight[0][:, cols].bitcast(weight[2]),
-                lhsT_scale=weight[1][:, cols],
-                rhs=moving[0][:].bitcast(moving[2]),
-                rhs_scale=moving[1][:],
-                start=start,
-                stop=not start,
-            )
+        def products(acc, weight, moving, s, opens):
+            slots = slice(s * JH, (s + 1) * JH)
+            for t in range(PACK):
+                cols = slice(t * P, (t + 1) * P)
+                nc.tensor.matmul_mx(
+                    out=acc[:, t, :],
+                    lhsT=weight[0][:, cols].bitcast(weight[2]),
+                    lhsT_scale=weight[1][:, cols],
+                    rhs=moving[0][:, slots].bitcast(moving[2]),
+                    rhs_scale=moving[1][:, slots],
+                    start=opens and t == 0,
+                    stop=not opens and t == PACK - 1,
+                )
 
-        a_ps = [psum.tile([P, J], F32, name="a%d" % t, tag="bank%d" % t) for t in range(PACK)]
-        b_ps = [psum.tile([P, J], F32, name="b%d" % t, tag="bank%d" % (PACK + t)) for t in range(PACK)]
-        for t in range(PACK):
-            product(a_ps[t], first, t, tokens, True)
-        for t in range(PACK):
-            product(b_ps[t], second, t, tokens, True)
+        a_ps = [psum.tile([P, PACK, JH], F32, name="a%d" % s) for s in range(2)]
+        b_ps = [psum.tile([P, PACK, JH], F32, name="b%d" % s) for s in range(2)]
+        for s in range(2):
+            products(a_ps[s], first, tokens, s, True)
+        for s in range(2):
+            products(b_ps[s], second, tokens, s, True)
 
-        hid = sb.tile([P, PACK, J], F32, name="hid")
+        gate = sb.tile([P, PACK, J], F32, name="gate")
         for t in range(PACK):
-            product(a_ps[t], second, t, notes, False)
-            product(b_ps[t], first, t, notes, False)
-            a_sb = sb.tile([P, J], F32, name="a_sb%d" % t)
-            nc.scalar.copy(a_sb[:], a_ps[t][:])
-            best = sb.tile([P, J], F32, name="best%d" % t)
-            nc.vector.tensor_tensor(best[:], b_ps[t][:], a_sb[:], ALU.max)
-            gate = sb.tile([P, J], F32, name="gate%d" % t)
             nc.scalar.activation(
-                out=gate[:], in_=tg_sb[t][:].indirect(idx3[:]), func=ACT.Sigmoid,
+                out=gate[:, t, :], in_=tg_sb[t][:].indirect(idx3[:]), func=ACT.Sigmoid,
                 bias=bg_sb[:, t : t + 1], scale=sg_sb[:, t : t + 1],
             )
-            nc.vector.tensor_tensor(hid[:, t, :], best[:], gate[:], ALU.mult)
+
+        best = []
+        for s in range(2):
+            products(a_ps[s], second, notes, s, False)
+            products(b_ps[s], first, notes, s, False)
+            a_sb = sb.tile([P, JH, PACK], F32, name="a_sb%d" % s)
+            nc.vector.tensor_copy(a_sb[:], a_ps[s][:].rearrange("p t j -> p j t"))
+            best.append(sb.tile([P, JH, PACK], F32, name="best%d" % s))
+            nc.vector.tensor_tensor(best[s][:], b_ps[s][:].rearrange("p t j -> p j t"), a_sb[:], ALU.max)
 
         p_sb = [sb.tile([P, J], F32, name="p_sb%d" % h) for h in range(2)]
         woven = [sb.tile([P, JH, PACK], BF16, name="woven%d" % s, align_bytes=64) for s in range(2)]
         for s in range(2):
-            nc.vector.tensor_copy(
-                woven[s][:].rearrange("p (c i) t -> p c t i", i=4),
-                hid[:, :, s * JH : (s + 1) * JH].rearrange("p t (c i) -> p c t i", i=4),
+            nc.vector.tensor_tensor(
+                woven[s][:], best[s][:],
+                gate[:, :, s * JH : (s + 1) * JH].rearrange("p t j -> p j t"), ALU.mult,
             )
         for s in range(2):
             codes = sb.tile([P, JH], U32, name="codes%d" % s, align_bytes=64)
@@ -176,7 +181,7 @@ def tile_list_crossed_tablegate_one_bestoftwo_kernel(
                 in_=woven[s][:].rearrange("p j t -> p (j t)"),
             )
             for h in range(2):
-                p_ps = psum.tile([P, JH], F32, name="p%d%d" % (s, h), tag="bank%d" % (2 * s + h))
+                p_ps = psum.tile([P, JH], F32, name="p%d%d" % (s, h))
                 nc.tensor.matmul_mx(
                     out=p_ps[:],
                     lhsT=wb_w[:, h * 2 * P : (h + 1) * 2 * P].bitcast(E2M1),

@@ -37,9 +37,9 @@ def tile_list_crossed_tablegate_one_bestoftwo_kernel(
             nc.sync.dma_start(tile[:], src)
             return tile
 
-        def scale_plane(width, name):
+        def scale_plane(engine, width, name):
             plane = sb.tile([P, width], U8, name=name, align_bytes=64)
-            nc.vector.memset(plane[:].bitcast(I32), 0)
+            engine.memset(plane[:].bitcast(I32), 0)
             return plane
 
         def load_scales(queue, plane, src, quads=range(4)):
@@ -69,11 +69,11 @@ def tile_list_crossed_tablegate_one_bestoftwo_kernel(
             queue.dma_start(tile[:], src.rearrange("(p t) o -> p (t o)", t=PACK))
             return tile
 
-        w2_s_raw = scale_plane(R, "w2_s_raw")
-        xt_s = scale_plane(T, "xt_s")
-        w_s_raw = scale_plane(R, "w_s_raw")
-        xo_s = scale_plane(Z, "xo_s")
-        wb_s = scale_plane(N, "wb_s")
+        xt_s = scale_plane(nc.gpsimd, T, "xt_s")
+        w2_s_raw = scale_plane(nc.gpsimd, R, "w2_s_raw")
+        w_s_raw = scale_plane(nc.vector, R, "w_s_raw")
+        xo_s = scale_plane(nc.vector, Z, "xo_s")
+        wb_s = scale_plane(nc.vector, N, "wb_s")
 
         load_scales(nc.gpsimd, w2_s_raw, w2_scales)
         idx = load_list(offs, "idx")
@@ -122,7 +122,12 @@ def tile_list_crossed_tablegate_one_bestoftwo_kernel(
         xo_gw = gather(xo_w, idx2, U32, "xo_gw")
         w2_w = deal(w2_w_raw, U32, "w2_w")
         w2_s = deal(w2_s_raw, U8, "w2_s", tag="w2_w_raw")
-        xo_gs = gather(xo_s, idx2, U8, "xo_gs")
+        xo_gs = sb.tile([P, J], U8, name="xo_gs", align_bytes=64)
+        for s in range(2):
+            nc.vector.tensor_copy(
+                xo_gs[:, s * JH : (s + 1) * JH],
+                xo_s[:].indirect(idx2[:, s * JH // 16 : (s + 1) * JH // 16]),
+            )
 
         first = (w_w, w_s, E4M3)
         second = (w2_w, w2_s, E5M2)
@@ -157,14 +162,14 @@ def tile_list_crossed_tablegate_one_bestoftwo_kernel(
                 bias=bg_sb[:, t : t + 1], scale=sg_sb[:, t : t + 1],
             )
 
-        best = []
-        for s in range(2):
+        a_sb = [sb.tile([P, JH, PACK], F32, name="a_sb%d" % s) for s in range(2)]
+        best = [sb.tile([P, JH, PACK], F32, name="best%d" % s) for s in range(2)]
+        for s, move in enumerate((nc.vector.tensor_copy, nc.vector.tensor_copy)):
             products(a_ps[s], second, notes, s, False)
+            move(a_sb[s][:], a_ps[s][:].rearrange("p t j -> p j t"))
+        for s in range(2):
             products(b_ps[s], first, notes, s, False)
-            a_sb = sb.tile([P, JH, PACK], F32, name="a_sb%d" % s)
-            nc.vector.tensor_copy(a_sb[:], a_ps[s][:].rearrange("p t j -> p j t"))
-            best.append(sb.tile([P, JH, PACK], F32, name="best%d" % s))
-            nc.vector.tensor_tensor(best[s][:], b_ps[s][:].rearrange("p t j -> p j t"), a_sb[:], ALU.max)
+            nc.vector.tensor_tensor(best[s][:], b_ps[s][:].rearrange("p t j -> p j t"), a_sb[s][:], ALU.max)
 
         p_sb = [sb.tile([P, J], F32, name="p_sb%d" % h) for h in range(2)]
         woven = [sb.tile([P, JH, PACK], BF16, name="woven%d" % s, align_bytes=64) for s in range(2)]

from contextlib import ExitStack

import concourse.mybir as mybir

F32 = mybir.dt.float32
BF16 = mybir.dt.bfloat16
I32 = mybir.dt.int32
U32 = mybir.dt.uint32
U16 = mybir.dt.uint16
U8 = mybir.dt.uint8
E4M3 = mybir.dt.float8_e4m3fn_x4
E5M2 = mybir.dt.float8_e5m2_x4
E2M1 = mybir.dt.float4_e2m1fn_x4
ACT = mybir.ActivationFunctionType
ALU = mybir.AluOpType

K, T, Z, J, R, Q, N, E = 512, 1024, 1024, 256, 512, 1024, 256, 128
P = 128
PACK = 4
JH = J // 2

FLOPS = 2 * (4 * K * R * J + R * N * J)


def tile_list_crossed_tablegate_one_bestoftwo_kernel(
    tc, xt_words, xt_scales, xo_words, xo_scales, w_words, w_scales, w2_words, w2_scales,
    tg, sg, bg, wb_words, wb_scales, offs, offs2, offs3, offs4, offs5, out,
):
    nc = tc.nc
    with ExitStack() as ctx:
        lists = ctx.enter_context(tc.tile_pool(name="lists", bufs=1))
        sb = ctx.enter_context(tc.tile_pool(name="sb", bufs=1))
        psum = ctx.enter_context(tc.psum_pool(name="psum", bufs=1))

        def load_list(src, name):
            tile = lists.tile(list(src.shape), U16, name=name)
            nc.sync.dma_start(tile[:], src)
            return tile

        def scale_plane(engine, width, name):
            plane = sb.tile([P, width], U8, name=name, align_bytes=64)
            engine.memset(plane[:].bitcast(I32), 0)
            return plane

        def load_scales(queue, plane, src, quads=range(4)):
            for quad in quads:
                queue.dma_start(
                    plane[32 * quad : 32 * quad + 4, :].bitcast(I32),
                    src[0, 4 * quad : 4 * quad + 4, :].bitcast(I32),
                )

        def load_words(queue, width, dtype, src, name):
            tile = sb.tile([P, width], dtype, name=name, align_bytes=64)
            queue.dma_start(tile[:].bitcast(I32), src.bitcast(I32))
            return tile

        def words32(src):
            return src[0].rearrange("p c b -> p (c b)")

        tg_rows = tg.rearrange("(p t) q -> p t q", t=PACK)
        tg_sb = [None] * PACK

        def load_tg(queue, t):
            tg_sb[t] = sb.tile([P, Q], F32, name="tg%d" % t)
            queue.dma_start(tg_sb[t][:], tg_rows[:, t, :])

        def load_col(queue, src, name):
            tile = sb.tile([P, PACK], F32, name=name)
            queue.dma_start(tile[:], src.rearrange("(p t) o -> p (t o)", t=PACK))
            return tile

        xt_s = scale_plane(nc.gpsimd, T, "xt_s")
        w2_s_raw = scale_plane(nc.gpsimd, R, "w2_s_raw")
        w_s_raw = scale_plane(nc.vector, R, "w_s_raw")
        xo_s = scale_plane(nc.vector, Z, "xo_s")
        wb_s = scale_plane(nc.vector, N, "wb_s")

        load_scales(nc.gpsimd, w2_s_raw, w2_scales)
        idx = load_list(offs, "idx")
        xt_w = load_words(nc.sync, T, U16, xt_words[0], "xt_w")
        load_scales(nc.sync, xt_s, xt_scales)
        w_w_raw = load_words(nc.sync, R, U32, words32(w_words), "w_w_raw")
        xo_w = load_words(nc.sync, Z, U32, words32(xo_words), "xo_w")
        load_scales(nc.sync, w_s_raw, w_scales)
        idx2 = load_list(offs2, "idx2")
        w2_w_raw = load_words(nc.sync, R, U32, words32(w2_words), "w2_w_raw")
        load_tg(nc.sync, 0)
        load_scales(nc.sync, xo_s, xo_scales)
        load_tg(nc.sync, 1)
        idx3 = load_list(offs3, "idx3")
        sg_sb = load_col(nc.sync, sg, "sg_sb")
        bg_sb = load_col(nc.sync, bg, "bg_sb")
        load_tg(nc.sync, 2)
        load_tg(nc.sync, 3)
        wb_w = load_words(nc.sync, 2 * N, U8, wb_words[0], "wb_w")
        load_scales(nc.sync, wb_s, wb_scales)
        idx4 = load_list(offs4, "idx4")
        idx5 = load_list(offs5, "idx5")

        warm_in = sb.tile([P, 1], F32, name="warm_in")
        warm_out = sb.tile([P, 1], F32, name="warm_out")
        nc.vector.memset(warm_in[:], 0.0)
        nc.scalar.activation(out=warm_out[:], in_=warm_in[:], func=ACT.Sigmoid)

        def gather(table, offsets, dtype, name):
            picked = sb.tile([P, J], dtype, name=name, align_bytes=64)
            nc.vector.tensor_copy(picked[:], table[:].indirect(offsets[:]))
            return picked

        def deal(raw, dtype, name, tag=None):
            dealt = sb.tile([P, R], dtype, name=name, tag=tag or name, align_bytes=64)
            nc.vector.tensor_copy(
                dealt[:].rearrange("p (t c i) -> p c t i", t=PACK, i=4),
                raw[:].rearrange("p (c i t) -> p c t i", t=PACK, i=4),
            )
            return dealt

        xt_gw = gather(xt_w, idx, U16, "xt_gw")
        xt_gs = gather(xt_s, idx, U8, "xt_gs")
        w_w = deal(w_w_raw, U32, "w_w")
        w_s = deal(w_s_raw, U8, "w_s")
        xo_gw = gather(xo_w, idx2, U32, "xo_gw")
        w2_w = deal(w2_w_raw, U32, "w2_w")
        w2_s = deal(w2_s_raw, U8, "w2_s", tag="w2_w_raw")
        xo_gs = sb.tile([P, J], U8, name="xo_gs", align_bytes=64)
        for s in range(2):
            nc.vector.tensor_copy(
                xo_gs[:, s * JH : (s + 1) * JH],
                xo_s[:].indirect(idx2[:, s * JH // 16 : (s + 1) * JH // 16]),
            )

        first = (w_w, w_s, E4M3)
        second = (w2_w, w2_s, E5M2)
        tokens = (xt_gw, xt_gs, E2M1)
        notes = (xo_gw, xo_gs, E4M3)

        def products(acc, weight, moving, s, opens):
            slots = slice(s * JH, (s + 1) * JH)
            for t in range(PACK):
                cols = slice(t * P, (t + 1) * P)
                nc.tensor.matmul_mx(
                    out=acc[:, t, :],
                    lhsT=weight[0][:, cols].bitcast(weight[2]),
                    lhsT_scale=weight[1][:, cols],
                    rhs=moving[0][:, slots].bitcast(moving[2]),
                    rhs_scale=moving[1][:, slots],
                    start=opens and t == 0,
                    stop=not opens and t == PACK - 1,
                )

        a_ps = [psum.tile([P, PACK, JH], F32, name="a%d" % s) for s in range(2)]
        b_ps = [psum.tile([P, PACK, JH], F32, name="b%d" % s) for s in range(2)]
        for s in range(2):
            products(a_ps[s], first, tokens, s, True)
        for s in range(2):
            products(b_ps[s], second, tokens, s, True)

        gate = sb.tile([P, PACK, J], F32, name="gate")
        for t in range(PACK):
            nc.scalar.activation(
                out=gate[:, t, :], in_=tg_sb[t][:].indirect(idx3[:]), func=ACT.Sigmoid,
                bias=bg_sb[:, t : t + 1], scale=sg_sb[:, t : t + 1],
            )

        a_sb = [sb.tile([P, JH, PACK], F32, name="a_sb%d" % s) for s in range(2)]
        best = [sb.tile([P, JH, PACK], F32, name="best%d" % s) for s in range(2)]
        for s, move in enumerate((nc.vector.tensor_copy, nc.vector.tensor_copy)):
            products(a_ps[s], second, notes, s, False)
            move(a_sb[s][:], a_ps[s][:].rearrange("p t j -> p j t"))
        for s in range(2):
            products(b_ps[s], first, notes, s, False)
            nc.vector.tensor_tensor(best[s][:], b_ps[s][:].rearrange("p t j -> p j t"), a_sb[s][:], ALU.max)

        p_sb = [sb.tile([P, J], F32, name="p_sb%d" % h) for h in range(2)]
        woven = [sb.tile([P, JH, PACK], BF16, name="woven%d" % s, align_bytes=64) for s in range(2)]
        for s in range(2):
            nc.vector.tensor_tensor(
                woven[s][:], best[s][:],
                gate[:, :, s * JH : (s + 1) * JH].rearrange("p t j -> p j t"), ALU.mult,
            )
        for s in range(2):
            codes = sb.tile([P, JH], U32, name="codes%d" % s, align_bytes=64)
            plane = sb.tile([P, JH], U8, name="plane%d" % s, align_bytes=64)
            nc.vector.quantize_mx(
                out=codes[:].bitcast(E5M2), scales=plane[:],
                in_=woven[s][:].rearrange("p j t -> p (j t)"),
            )
            for h in range(2):
                p_ps = psum.tile([P, JH], F32, name="p%d%d" % (s, h))
                nc.tensor.matmul_mx(
                    out=p_ps[:],
                    lhsT=wb_w[:, h * 2 * P : (h + 1) * 2 * P].bitcast(E2M1),
                    lhsT_scale=wb_s[:, h * P : (h + 1) * P],
                    rhs=codes[:].bitcast(E5M2),
                    rhs_scale=plane[:],
                    start=True,
                    stop=True,
                )
                dst = p_sb[h][:, s * JH : (s + 1) * JH]
                if s == 1 and h == 1:
                    nc.vector.tensor_copy(dst, p_ps[:])
                else:
                    nc.scalar.copy(dst, p_ps[:])

        for h in (1, 0):
            picks = []
            for k, offsets in enumerate((idx4, idx5)):
                pick = sb.tile([P, E], F32, name="pick%d%d" % (h, k))
                if h == 0:
                    nc.scalar.activation(out=pick[:], in_=p_sb[h][:].indirect(offsets[:]), func=ACT.Copy)
                else:
                    nc.vector.tensor_copy(pick[:], p_sb[h][:].indirect(offsets[:]))
                picks.append(pick)
            res = sb.tile([P, E], F32, name="res%d" % h)
            nc.vector.tensor_tensor(res[:], picks[0][:], picks[1][:], ALU.max)
            nc.sync.dma_start(out[h * P : (h + 1) * P, :], res[:])
